import numpy as np
import ml_dtypes


def mxq(x, axis, fmt="e4m3"):
    dtype, down = {"e4m3": (ml_dtypes.float8_e4m3fn, 7), "e5m2": (ml_dtypes.float8_e5m2, 14)}[fmt]
    v = np.moveaxis(np.asarray(x, np.float32).astype(ml_dtypes.bfloat16).astype(np.float64), axis, -1)
    blocks = v.reshape(v.shape[:-1] + (-1, 32))
    amax = np.abs(blocks).max(-1, keepdims=True)
    byte = np.maximum(np.where(amax > 0, np.frexp(amax)[1] - 1 + 127, 0) - down, 1)
    scale = np.exp2(byte - 127.0)
    codes = (blocks / scale).astype(np.float32).astype(dtype).astype(np.float64)
    return np.moveaxis((codes * scale).reshape(v.shape), -1, axis)


WIDE = False


def mx_kscale(k):
    if not WIDE:
        return np.ones(k)
    levels = np.array([10, -10, 5, -5, 0])
    if k % 512:
        return np.exp2(np.random.permutation(np.resize(levels, k // 32))).repeat(32)
    a = np.empty((k // 512, 16))
    for p in range(k // 512):
        a[p, :8] = np.random.permutation(np.resize(levels, 8))
        for g in range(8):
            far = levels[np.abs(levels - a[p, g]) >= 10]
            a[p, g + 8] = far[np.random.randint(len(far))]
    return np.exp2(a.ravel()).repeat(32)


BF16 = ml_dtypes.bfloat16


def bf(x):
    return np.asarray(x, np.float32).astype(BF16)


def f64(x):
    return np.asarray(x).astype(np.float64)


E2M1 = np.array([0.0, 0.5, 1.0, 1.5, 2.0, 3.0, 4.0, 6.0, -0.0, -0.5, -1.0, -1.5, -2.0, -3.0, -4.0, -6.0])


def pack_weight(w, fmt):
    k, n = w.shape
    w = f64(bf(w)).reshape(k // 32, 32, n)
    amax = np.abs(w).max(1)
    if fmt == "e4m3":
        byte = np.frexp(amax)[1] - 1 + 127 - 7
    else:
        mant, ex = np.frexp(amax / 6.0)
        byte = np.where(mant > 0.5, ex, ex - 1) + 127
    byte = np.clip(np.where(amax > 0, byte, 1), 1, 254)
    scaled = (w * np.exp2(127.0 - byte)[:, None, :]).reshape(k, n).astype(np.float32)
    by_word = np.ascontiguousarray(scaled.reshape(k // 512, 128, 4, n).transpose(0, 1, 3, 2))
    if fmt == "e4m3":
        words = by_word.astype(ml_dtypes.float8_e4m3fn).view(np.uint8)
    else:
        c = by_word.astype(ml_dtypes.float4_e2m1fn).view(np.uint8) & 0xF
        words = c[..., 0::2] | (c[..., 1::2] << 4)
    return np.ascontiguousarray(words), np.ascontiguousarray(byte.astype(np.uint8).reshape(k // 512, 16, n))


def unpack_weight(words, scales, fmt):
    g, p, n, _ = words.shape
    if fmt == "e4m3":
        vals = np.ascontiguousarray(words).view(ml_dtypes.float8_e4m3fn).astype(np.float64)
    else:
        nib = np.empty((g, p, n, 4), np.uint8)
        nib[..., 0::2] = words & 0xF
        nib[..., 1::2] = words >> 4
        vals = E2M1[nib]
    vals = vals * np.repeat(np.exp2(scales.astype(np.float64) - 127.0), 8, axis=1)[..., None]
    return vals.transpose(0, 1, 3, 2).reshape(g * 512, n)
def pack4(w):
    words, scales = pack_weight(w, "e2m1")
    return words.reshape(words.shape[0], 128, -1), scales


def unpack4(words, scales):
    return unpack_weight(words.reshape(words.shape[0], 128, -1, 2), scales, "e2m1")


E4M3FN = np.array([(-1.0 if i & 128 else 1.0) * ((1.0 + (i & 7) / 8.0) * 2.0 ** (((i >> 3) & 15) - 7) if i & 120 else (i & 7) * 2.0 ** -9) for i in range(256)])


def e4m3fn_bytes(y):
    return np.clip(np.asarray(y, np.float64), -448.0, 448.0).astype(np.float32).astype(ml_dtypes.float8_e4m3fn).view(np.uint8)


def e4m3fn_values(b):
    return E4M3FN[b]


N, E, O, Q, TRIPLES, PER, BITS = 1024, 4, 512, 512, 3, 3, 2
J = TRIPLES * PER
NV = BITS**J
EO = E * O


def calibrate(x, cal):
    low = np.minimum(2.0 * x, 1.0)
    high = np.maximum(2.0 * x - 1.0, 0.0)
    return cal * low + (1.0 - cal) * high


def outer3(a, b, d):
    full = a[..., :, None, None] * b[..., None, :, None] * d[..., None, None, :]
    return full.reshape(a.shape[:-1] + (-1,))


def draw0():
    ks, kt = mx_kscale(NV), mx_kscale(EO)
    inputs = {
        "x": bf(np.random.uniform(0.02, 0.98, (N, E, J))),
        "cal": bf(np.random.uniform(0.2, 0.8, (E, J))),
        "g": bf(12.0 * np.random.standard_normal((E, NV)) * ks),
        "theta": bf(0.5 * np.random.standard_normal((E, NV, O)) / ks[:, None]),
        "s": bf((1.0 + 0.1 * np.random.standard_normal(EO)) * kt),
    }
    words, scales = pack4(2.0 * np.random.standard_normal((EO, Q)) / np.sqrt(EO) / kt[:, None])
    inputs["v_words"] = words
    inputs["v_scales"] = scales
    return inputs


def core(x, cal, g, theta, s, v_words, v_scales):
    x, cal, g, theta, s = f64(x), f64(cal), f64(g), f64(theta), f64(s)
    n, e, _ = x.shape

    u = calibrate(x, cal)
    p = np.stack([1.0 - u, u], axis=-1)

    p = p.reshape(n, e, TRIPLES, PER, BITS)
    t = outer3(p[:, :, :, 0, :], p[:, :, :, 1, :], p[:, :, :, 2, :])

    w = outer3(t[:, :, 0, :], t[:, :, 1, :], t[:, :, 2, :])

    wg = w * g

    l = mxq(wg.transpose(1, 0, 2), 2, "e4m3") @ mxq(theta, 1, "e4m3")

    h = np.tanh(l)
    flat = h.transpose(1, 0, 2).reshape(n, -1)

    f = flat * s

    return mxq(f, 1, "e4m3") @ unpack4(v_words, v_scales)


def setup_inputs():
    drawn = draw0()
    full = np.asarray(drawn['theta']).astype(np.float64)
    scale = (np.abs(full).reshape(4, 4, 128, 4, 128).max(axis=(2, 4)) / 448.0).astype(np.float32)
    given = {}
    for key, value in drawn.items():
        if key == 'theta':
            given['theta_bytes'] = e4m3fn_bytes(full / np.repeat(np.repeat(scale.astype(np.float64), 128, axis=1), 128, axis=2))
            given['theta_scale'] = scale
        else:
            given[key] = value
    return given


def reference(x, cal, g, theta_bytes, theta_scale, s, v_words, v_scales):
    return core(x, cal, g, e4m3fn_values(theta_bytes) * np.repeat(np.repeat(theta_scale.astype(np.float64), 128, axis=1), 128, axis=2), s, v_words, v_scales)

@@ -1,0 +1,418 @@
+from contextlib import ExitStack
+
+import concourse.mybir as mybir
+from concourse.masks import make_identity
+
+F32 = mybir.dt.float32
+BF16 = mybir.dt.bfloat16
+I32 = mybir.dt.int32
+U32 = mybir.dt.uint32
+U8 = mybir.dt.uint8
+F8 = mybir.dt.float8_e4m3fn
+FP8X4 = mybir.dt.float8_e4m3fn_x4
+FP4X4 = mybir.dt.float4_e2m1fn_x4
+ALU = mybir.AluOpType
+ACT = mybir.ActivationFunctionType
+AX = mybir.AxisListType
+
+N, E, J, NV, O, Q = 1024, 4, 9, 512, 512, 512
+FLOPS = 2 * N * E * NV * O + 2 * N * E * O * Q
+P = 128
+NT = N // P
+HALF = 4
+UNITS = [(0, 0), (1, 0), (0, 1), (2, 0), (3, 0), (1, 1), (2, 1), (3, 1)]
+LAST = 3
+
+
+def tile_calibratedlatticeensemble_d2p_kernel(
+    tc, x, cal, g, theta_bytes, theta_scale, s, v_words, v_scales, out
+):
+    nc = tc.nc
+    out_tiles = out.rearrange("(p a) q -> a p q", a=NT)
+
+    with ExitStack() as ctx:
+        keep = ctx.enter_context(tc.tile_pool(name="keep", bufs=1))
+        work = ctx.enter_context(tc.tile_pool(name="work", bufs=2))
+        psum = ctx.enter_context(tc.psum_pool(name="psum", bufs=1))
+
+        x_t = keep.tile([P, NT * E * J], BF16, name="x_t")
+        cal_t = keep.tile([P, E * J], BF16, name="cal_t")
+        ts_t = keep.tile([P, E, 4], F32, name="ts_t")
+        gk = keep.tile([P, NV], BF16, name="gk")
+        s_b = keep.tile([P, E, 4], BF16, name="s_b")
+        g3_b = keep.tile([P, 4], BF16, name="g3_b")
+        vw = keep.tile([P, E, 2 * Q], U8, name="vw", align_bytes=64)
+        vs = keep.tile([P, E, Q], U8, name="vs", align_bytes=64)
+        tb = [keep.tile([P, 4 * O], U8, name="tb%d" % e, align_bytes=64) for e in range(E)]
+
+        warm = keep.tile([P, 1], F32, name="warm")
+        warm2 = keep.tile([P, 1], F32, name="warm2")
+        bs = keep.tile([P, NT, P], BF16, name="bs")
+        ident = keep.tile([P, P], F32, name="ident")
+        ident_b = keep.tile([P, P], BF16, name="ident_b")
+        mask = keep.tile([P, 3, 4], F32, name="mask")
+        gt = keep.tile([P, 3, 4, P], BF16, name="gt")
+        s_f = keep.tile([P, E, 4], F32, name="s_f")
+        g3 = keep.tile([P, 4], F32, name="g3")
+
+        nc.sync.dma_start(out=x_t[:], in_=x.rearrange("(p a) e j -> p (a e j)", a=NT))
+        nc.sync.dma_start(out=cal_t[:], in_=cal.rearrange("e j -> (e j)").partition_broadcast(P))
+
+        def load_theta(e):
+            nc.sync.dma_start(out=tb[e][:], in_=theta_bytes[e].rearrange("(p t) o -> p (t o)", t=4))
+
+        load_theta(0)
+        for q in range(4):
+            nc.sync.dma_start(out=ts_t[32 * q : 32 * q + 32], in_=theta_scale[:, q, :].partition_broadcast(32))
+
+        nc.vector.memset(warm[:], 0.0)
+        nc.vector.memset(gk[:], 0.0)
+        nc.vector.memset(bs[:], 0.0)
+        for e in range(3):
+            nc.scalar.dma_start(out=gk[12 * e : 12 * e + 12, :], in_=g[e].partition_broadcast(12))
+        nc.scalar.activation(out=warm2[:], in_=warm[:], func=ACT.Tanh)
+        nc.sync.dma_start(out=s_b[:], in_=s.rearrange("(e p t) -> p e t", p=P, t=4))
+        nc.sync.dma_start(out=g3_b[:], in_=g[LAST].rearrange("(p t) -> p t", t=4))
+        for e in (1, 2, 3):
+            load_theta(e)
+        nc.sync.dma_start(out=vw[:], in_=v_words.rearrange("g p n -> p g n"))
+
+        make_identity(nc, ident[:])
+        nc.gpsimd.memset(vs[:].rearrange("p g n -> p (g n)").bitcast(I32), 0)
+        for q in range(4):
+            nc.sync.dma_start(
+                out=vs[32 * q : 32 * q + 4].bitcast(I32),
+                in_=v_scales[:, 4 * q : 4 * q + 4, :].bitcast(I32).rearrange("g r n -> r g n"),
+            )
+
+        tw = {}
+        ti = {}
+        thq = {}
+        ths = {}
+
+        def widen(e, t):
+            if t == 0:
+                tw[e] = work.tile([P, 4, O], BF16, tag="tw", name="tw%d" % e)
+            for j in range(4):
+                nc.scalar.activation(
+                    out=tw[e][:, t, P * j : P * (j + 1)],
+                    in_=tb[e][:, O * t + P * j : O * t + P * (j + 1)].bitcast(F8),
+                    func=ACT.Copy,
+                    scale=ts_t[:, e, j : j + 1],
+                )
+
+        def interleave(e, u, eng):
+            if u == 0:
+                ti[e] = work.tile([P, 4, P, 4], BF16, tag="ti", name="ti%d" % e, align_bytes=64)
+            src = tw[e][:].rearrange("p t (m u) -> p u m t", u=4)[:, u]
+            if eng == "v":
+                nc.vector.tensor_copy(out=ti[e][:, u], in_=src)
+            else:
+                nc.scalar.copy(out=ti[e][:, u], in_=src)
+
+        def quantize_theta(e):
+            thq[e] = keep.tile([P, O], U32, name="thq%d" % e, align_bytes=64)
+            ths[e] = keep.tile([P, O], U8, name="ths%d" % e, align_bytes=64)
+            nc.vector.quantize_mx(
+                out=thq[e][:].bitcast(FP8X4),
+                scales=ths[e][:],
+                in_=ti[e][:].rearrange("p u m t -> p (u m t)"),
+            )
+
+        cc = keep.tile([P, 2, E * J], F32, name="cc")
+        lh = keep.tile([P, 2, NT, E * J], F32, name="lh")
+        mm = keep.tile([P, 2, NT * E, J], F32, name="mm")
+        pl = keep.tile([P, 2, J, NT * E], F32, name="pl")
+        pp = keep.tile([P, 4 * NT * E, 4], F32, name="pp")
+        t0 = keep.tile([P, NT, E, 8], F32, name="t0")
+        t1 = keep.tile([P, NT, E, 16], F32, name="t1")
+        r1 = keep.tile([P, NT, 3, 4], F32, name="r1")
+        r2 = keep.tile([P, NT, 3, 4], F32, name="r2")
+
+        nc.vector.tensor_copy(out=ident_b[:], in_=ident[:])
+        nc.vector.tensor_reduce(
+            out=mask[:], in_=ident[:, 0:36].rearrange("p (e s t) -> p e t s", e=3, s=3), axis=AX.X, op=ALU.add
+        )
+        nc.vector.tensor_copy(out=cc[:, 0], in_=cal_t[:])
+        nc.vector.tensor_scalar(out=cc[:, 1], in0=cal_t[:], scalar1=-1.0, scalar2=1.0, op0=ALU.mult, op1=ALU.add)
+        for e in range(3):
+            nc.gpsimd.tensor_tensor(
+                out=gt[:, e],
+                in0=gk[:].rearrange("p (m t) -> p t m", t=4),
+                in1=mask[:, e].unsqueeze(2).to_broadcast([P, 4, P]),
+                op=ALU.mult,
+            )
+
+        xv = x_t[:].rearrange("p (a k) -> p a k", a=NT)
+        nc.vector.tensor_scalar(out=lh[:, 0], in0=xv, scalar1=2.0, scalar2=1.0, op0=ALU.mult, op1=ALU.min)
+        nc.vector.scalar_tensor_tensor(out=lh[:, 1], in0=xv, scalar=2.0, in1=lh[:, 0], op0=ALU.mult, op1=ALU.subtract)
+        nc.vector.tensor_tensor(
+            out=mm[:].rearrange("p b (a e) j -> p b a (e j)", a=NT),
+            in0=lh[:],
+            in1=cc[:].unsqueeze(2).to_broadcast([P, 2, NT, E * J]),
+            op=ALU.mult,
+        )
+        mj = mm[:].rearrange("p b r j -> p b j r")
+        nc.vector.tensor_tensor(out=pl[:, 1, 0:4], in0=mj[:, 0, 1:9:2], in1=mj[:, 1, 1:9:2], op=ALU.add)
+        nc.vector.tensor_tensor(out=pl[:, 1, 4:9], in0=mj[:, 0, 0:9:2], in1=mj[:, 1, 0:9:2], op=ALU.add)
+        nc.vector.tensor_scalar(out=pl[:, 0], in0=pl[:, 1], scalar1=-1.0, scalar2=1.0, op0=ALU.mult, op1=ALU.add)
+        first = pl[:, :, 0:4, :].rearrange("p b q r -> p (q r) b")
+        second = pl[:, :, 5:9, :].rearrange("p b q r -> p (q r) b")
+        nc.vector.tensor_tensor(
+            out=pp[:].rearrange("p r (a b) -> p r a b", a=2),
+            in0=first.unsqueeze(3).to_broadcast([P, P, 2, 2]),
+            in1=second.unsqueeze(2).to_broadcast([P, P, 2, 2]),
+            op=ALU.mult,
+        )
+        pq = pp[:].rearrange("p (q r) c -> p q r c", q=4)
+        tail_pair = pq[:, 3].rearrange("p (a e) t -> p a e t", a=NT)
+        bsv = bs[:, :, 0:36].rearrange("p a (e s t) -> p a e s t", e=3, s=3)
+        nc.vector.tensor_copy(out=bsv[:, :, :, 0, :], in_=tail_pair[:, :, 0:3])
+        nc.vector.tensor_tensor(
+            out=t0[:].rearrange("p a e (b c) -> p (a e) b c", b=2),
+            in0=pl[:, :, 4, :].rearrange("p b r -> p r b").unsqueeze(3).to_broadcast([P, NT * E, 2, 4]),
+            in1=pq[:, 0].unsqueeze(2).to_broadcast([P, NT * E, 2, 4]),
+            op=ALU.mult,
+        )
+        nc.vector.tensor_tensor(out=r1[:], in0=tail_pair[:, :, 0:3], in1=bsv[:, :, :, 0, :], op=ALU.subtract)
+        nc.vector.tensor_tensor(
+            out=t1[:].rearrange("p a e (b c) -> p (a e) b c", b=4),
+            in0=pq[:, 1].unsqueeze(3).to_broadcast([P, NT * E, 4, 4]),
+            in1=pq[:, 2].unsqueeze(2).to_broadcast([P, NT * E, 4, 4]),
+            op=ALU.mult,
+        )
+        nc.vector.tensor_copy(out=bsv[:, :, :, 1, :], in_=r1[:])
+
+        a_t = {}
+
+        def product(k):
+            e, h = UNITS[k]
+            rows = slice(HALF * h, HALF * h + HALF)
+            a_t[k] = work.tile([P, HALF, P], F32, tag="a", name="a%d" % k)
+            nc.vector.tensor_tensor(
+                out=a_t[k][:].rearrange("p a (b c) -> p a b c", b=8),
+                in0=t0[:, rows, e, :].unsqueeze(3).to_broadcast([P, HALF, 8, 16]),
+                in1=t1[:, rows, e, :].unsqueeze(2).to_broadcast([P, HALF, 8, 16]),
+                op=ALU.mult,
+            )
+
+        product(0)
+        nc.vector.tensor_tensor(out=r2[:], in0=r1[:], in1=bsv[:, :, :, 1, :], op=ALU.subtract)
+        nc.vector.tensor_copy(out=bsv[:, :, :, 2, :], in_=r2[:])
+
+        for t in range(4):
+            widen(0, t)
+        for u in range(4):
+            interleave(0, u, "v")
+        product(1)
+
+        bt = keep.tile([P, N], BF16, name="bt")
+        at = {}
+
+        def turn(k):
+            tp = psum.tile([P, HALF, P], F32, tag="pa", name="pa%d" % k, bufs=1)
+            for i in range(HALF):
+                nc.tensor.transpose(tp[:, i, :], a_t[k][:, i, :], ident[:])
+            return tp
+
+        def empty(k, tp):
+            e, h = UNITS[k]
+            flat = tp[:].rearrange("p a r -> p (a r)")
+            if e != LAST:
+                at[k] = work.tile([P, HALF * P], F32, tag="at", name="at%d" % k)
+                nc.scalar.copy(out=at[k][:], in_=flat)
+            else:
+                at[k] = work.tile([P, 4, HALF * P], F32, tag="at3", name="at%d" % k)
+                for t in range(4):
+                    nc.scalar.activation(out=at[k][:, t], in_=flat, func=ACT.Copy, scale=g3[:, t : t + 1])
+
+        empty(0, turn(0))
+        for h in range(2):
+            btp = psum.tile([P, HALF, P], BF16, tag="po", name="btp%d" % h, bufs=2)
+            for i in range(HALF):
+                nc.tensor.transpose(btp[:, i, :], bs[:, HALF * h + i, :], ident_b[:])
+            nc.scalar.copy(out=bt[:, HALF * P * h : HALF * P * (h + 1)], in_=btp[:].rearrange("p a r -> p (a r)"))
+
+        cb = {}
+
+        def spread(k, i):
+            e, h = UNITS[k]
+            a = HALF * h + i
+            cb[(k, i)] = psum.tile([P, 4, P], F32, tag="pc", name="pc%d_%d" % (k, i), bufs=3)
+            for t in range(4):
+                if e != LAST:
+                    nc.tensor.matmul(
+                        cb[(k, i)][:, t, :],
+                        lhsT=gt[:, e, t, :],
+                        rhs=bt[:, P * a : P * (a + 1)],
+                        start=True,
+                        stop=True,
+                    )
+                else:
+                    nc.tensor.transpose(
+                        cb[(k, i)][:, t, :], tail_pair[:, a, e, t : t + 1].to_broadcast([P, P]), ident[:]
+                    )
+
+        wg = {}
+        wq = {}
+        wsc = {}
+        hh = {}
+        ff = {}
+        fq = {}
+        fs = {}
+
+        def weight(k, i):
+            e, h = UNITS[k]
+            if i == 0:
+                wg[k] = work.tile([P, HALF, P, 4], BF16, tag="wg", name="wg%d" % k, align_bytes=64)
+            cols = slice(P * i, P * (i + 1))
+            if e != LAST:
+                right = at[k][:, cols].unsqueeze(2).to_broadcast([P, P, 4])
+            else:
+                right = at[k][:, :, cols].rearrange("p t r -> p r t")
+            nc.vector.tensor_tensor(
+                out=wg[k][:, i], in0=cb[(k, i)][:].rearrange("p t r -> p r t"), in1=right, op=ALU.mult
+            )
+
+        def quantize_weight(k):
+            wq[k] = work.tile([P, HALF * P], U32, tag="wq", name="wq%d" % k, align_bytes=64)
+            wsc[k] = work.tile([P, HALF * P], U8, tag="wsc", name="wsc%d" % k, align_bytes=64)
+            nc.vector.quantize_mx(
+                out=wq[k][:].bitcast(FP8X4), scales=wsc[k][:], in_=wg[k][:].rearrange("p a r t -> p (a r t)")
+            )
+
+        def lattice(k, i):
+            e, h = UNITS[k]
+            lb = psum.tile([P, 4, P], F32, tag="pl", name="pl%d_%d" % (k, i), bufs=2)
+            cols = slice(P * i, P * (i + 1))
+            for u in range(4):
+                nc.tensor.matmul_mx(
+                    out=lb[:, u, :],
+                    lhsT=thq[e][:, P * u : P * (u + 1)].bitcast(FP8X4),
+                    lhsT_scale=ths[e][:, P * u : P * (u + 1)],
+                    rhs=wq[k][:, cols].bitcast(FP8X4),
+                    rhs_scale=wsc[k][:, cols],
+                    start=True,
+                    stop=True,
+                )
+            if i == 0:
+                hh[k] = work.tile([P, HALF, P, 4], F32, tag="hh", name="hh%d" % k)
+            nc.scalar.activation(out=hh[k][:, i], in_=lb[:].rearrange("p t r -> p r t"), func=ACT.Tanh)
+
+        def gain(k, i0, i1):
+            e, h = UNITS[k]
+            if i0 == 0:
+                ff[k] = work.tile([P, HALF, P, 4], BF16, tag="ff", name="ff%d" % k, align_bytes=64)
+                fq[k] = keep.tile([P, HALF * P], U32, name="fq%d" % k, align_bytes=64)
+                fs[k] = keep.tile([P, HALF * P], U8, name="fs%d" % k, align_bytes=64)
+            n = (i1 - i0) * P
+            nc.vector.tensor_tensor(
+                out=ff[k][:, i0:i1].rearrange("p a r t -> p (a r) t"),
+                in0=hh[k][:, i0:i1].rearrange("p a r t -> p (a r) t"),
+                in1=s_f[:, e, :].unsqueeze(1).to_broadcast([P, n, 4]),
+                op=ALU.mult,
+            )
+
+        def quantize_gain(k, i0, i1):
+            nc.vector.quantize_mx(
+                out=fq[k][:, P * i0 : P * i1].bitcast(FP8X4),
+                scales=fs[k][:, P * i0 : P * i1],
+                in_=ff[k][:, i0:i1].rearrange("p a r t -> p (a r t)"),
+            )
+
+        unit_of = {UNITS[k]: k for k in range(len(UNITS))}
+
+        def mix(ob, e, a):
+            k = unit_of[(e, a // HALF)]
+            cols = slice(P * (a % HALF), P * (a % HALF + 1))
+            nc.tensor.matmul_mx(
+                out=ob[:],
+                lhsT=fq[k][:, cols].bitcast(FP8X4),
+                lhsT_scale=fs[k][:, cols],
+                rhs=vw[:, e, :].bitcast(FP4X4),
+                rhs_scale=vs[:, e, :],
+                start=(e == 0),
+                stop=(e == E - 1),
+            )
+
+        def leave(ob, a, eng):
+            res = work.tile([P, Q], F32, tag="res", name="res%d" % a, bufs=4)
+            if eng == "v":
+                nc.vector.tensor_copy(out=res[:], in_=ob[:])
+            else:
+                nc.scalar.copy(out=res[:], in_=ob[:])
+            nc.sync.dma_start(out=out_tiles[a], in_=res[:])
+
+        nc.vector.tensor_copy(out=s_f[:], in_=s_b[:])
+        nc.vector.tensor_copy(out=g3[:], in_=g3_b[:])
+        quantize_theta(0)
+
+        order = [(k, i) for k in range(8) for i in range(HALF)]
+        for n in range(3):
+            spread(order[n][0], order[n][1])
+
+        for t in range(4):
+            widen(1, t)
+        scalar_work = {
+            0: [("i", 1, 0), ("i", 1, 1), ("i", 1, 2), ("i", 1, 3), ("w", 2, 0), ("w", 2, 1)],
+            1: [("w", 2, 2), ("w", 2, 3), ("i", 2, 0), ("i", 2, 1)],
+            2: [("i", 2, 2), ("i", 2, 3), ("w", 3, 0), ("w", 3, 1), ("w", 3, 2), ("w", 3, 3)],
+            3: [("i", 3, 0), ("i", 3, 1), ("i", 3, 2), ("i", 3, 3)],
+        }
+        theta_at = {1: 1, 3: 2, 4: 3}
+
+        late = {}
+        for st in range(9):
+            if st + 1 < 8:
+                tp = turn(st + 1)
+            for i in range(HALF):
+                if st < 8:
+                    weight(st, i)
+                if st >= 1:
+                    lattice(st - 1, i)
+                n = HALF * st + i + 3
+                if n < 32:
+                    spread(order[n][0], order[n][1])
+                if st in (6, 7) and i % 2 == 1:
+                    a = 2 * (st - 6) + i // 2
+                    ob = psum.tile([P, Q], F32, tag="po", name="po%d" % a, bufs=2)
+                    for e in range(E):
+                        mix(ob, e, a)
+                    leave(ob, a, "s")
+                if st == 0 and i == 0:
+                    empty(1, tp)
+            if st >= 1 and st + 1 < 8:
+                empty(st + 1, tp)
+            for kind, e, part in scalar_work.get(st, []):
+                if kind == "w":
+                    widen(e, part)
+                else:
+                    interleave(e, part, "s")
+            if st + 2 < 8:
+                product(st + 2)
+            if st >= 1 and st < 8:
+                gain(st - 1, 0, 2)
+                gain(st - 1, 2, 4)
+            if st in theta_at:
+                quantize_theta(theta_at[st])
+            if st < 8:
+                quantize_weight(st)
+            if st >= 1 and st < 8:
+                quantize_gain(st - 1, 0, 4)
+
+        for i in range(HALF):
+            gain(7, i, i + 1)
+            if i >= 1:
+                quantize_gain(7, i - 1, i)
+        quantize_gain(7, 3, 4)
+        tags = ["po", "po", "pa", "pc"]
+        depth = {"po": 2, "pa": 1, "pc": 3}
+        for i in range(HALF):
+            a = HALF + i
+            late[a] = psum.tile([P, Q], F32, tag=tags[i], name="po%d" % a, bufs=depth[tags[i]])
+            for e in range(3):
+                mix(late[a], e, a)
+        for i in range(HALF):
+            a = HALF + i
+            mix(late[a], 3, a)
+            leave(late[a], a, "s" if i % 2 == 0 else "v")

@@ -13,15 +13,18 @@ FP8X4 = mybir.dt.float8_e4m3fn_x4
 FP4X4 = mybir.dt.float4_e2m1fn_x4
 ALU = mybir.AluOpType
 ACT = mybir.ActivationFunctionType
-AX = mybir.AxisListType
 
 N, E, J, NV, O, Q = 1024, 4, 9, 512, 512, 512
 FLOPS = 2 * N * E * NV * O + 2 * N * E * O * Q
 P = 128
 NT = N // P
 HALF = 4
-UNITS = [(0, 0), (1, 0), (0, 1), (2, 0), (3, 0), (1, 1), (2, 1), (3, 1)]
+UNITS = [(0, 0), (1, 0), (0, 1), (3, 0), (2, 0), (1, 1), (3, 1), (2, 1)]
 LAST = 3
+PASSES = [0, 1, 3, 2]
+GPS_PRODUCT = ()
+THETA0 = "v"
+WHO = {1: "g", 2: "s", 3: "s"}
 
 
 def tile_calibratedlatticeensemble_d2p_kernel(
@@ -34,46 +37,44 @@ def tile_calibratedlatticeensemble_d2p_kernel(
         keep = ctx.enter_context(tc.tile_pool(name="keep", bufs=1))
         work = ctx.enter_context(tc.tile_pool(name="work", bufs=2))
         psum = ctx.enter_context(tc.psum_pool(name="psum", bufs=1))
-
-        x_t = keep.tile([P, NT * E * J], BF16, name="x_t")
+        ctx.enter_context(tc.manual_schedule())
+        x_t = keep.tile([P, NT, E * J], BF16, name="x_t")
         cal_t = keep.tile([P, E * J], BF16, name="cal_t")
         ts_t = keep.tile([P, E, 4], F32, name="ts_t")
-        gk = keep.tile([P, NV], BF16, name="gk")
         s_b = keep.tile([P, E, 4], BF16, name="s_b")
-        g3_b = keep.tile([P, 4], BF16, name="g3_b")
+        g_b = keep.tile([P, E, 4], BF16, name="g_b")
         vw = keep.tile([P, E, 2 * Q], U8, name="vw", align_bytes=64)
         vs = keep.tile([P, E, Q], U8, name="vs", align_bytes=64)
         tb = [keep.tile([P, 4 * O], U8, name="tb%d" % e, align_bytes=64) for e in range(E)]
 
         warm = keep.tile([P, 1], F32, name="warm")
         warm2 = keep.tile([P, 1], F32, name="warm2")
-        bs = keep.tile([P, NT, P], BF16, name="bs")
+        bs = [keep.tile([P, HALF, 4 * 131], BF16, name="bs%d" % h) for h in range(2)]
+        glt = keep.tile([P, 3 * 140], BF16, name="glt")
         ident = keep.tile([P, P], F32, name="ident")
         ident_b = keep.tile([P, P], BF16, name="ident_b")
-        mask = keep.tile([P, 3, 4], F32, name="mask")
-        gt = keep.tile([P, 3, 4, P], BF16, name="gt")
+        gl = keep.tile([P, 3, P], BF16, name="gl")
         s_f = keep.tile([P, E, 4], F32, name="s_f")
         g3 = keep.tile([P, 4], F32, name="g3")
 
-        nc.sync.dma_start(out=x_t[:], in_=x.rearrange("(p a) e j -> p (a e j)", a=NT))
-        nc.sync.dma_start(out=cal_t[:], in_=cal.rearrange("e j -> (e j)").partition_broadcast(P))
+        nc.sync.dma_start(out=x_t[:], in_=x.rearrange("(p a) e j -> p a (e j)", a=NT))
+        nc.scalar.dma_start(out=cal_t[:], in_=cal.rearrange("e j -> (e j)").partition_broadcast(P))
 
         def load_theta(e):
             nc.sync.dma_start(out=tb[e][:], in_=theta_bytes[e].rearrange("(p t) o -> p (t o)", t=4))
 
-        load_theta(0)
         for q in range(4):
             nc.sync.dma_start(out=ts_t[32 * q : 32 * q + 32], in_=theta_scale[:, q, :].partition_broadcast(32))
+        load_theta(0)
+        nc.scalar.dma_start(out=g_b[:], in_=g.rearrange("e (p t) -> p e t", t=4))
 
         nc.vector.memset(warm[:], 0.0)
-        nc.vector.memset(gk[:], 0.0)
-        nc.vector.memset(bs[:], 0.0)
-        for e in range(3):
-            nc.scalar.dma_start(out=gk[12 * e : 12 * e + 12, :], in_=g[e].partition_broadcast(12))
+        nc.vector.memset(glt[:], 0.0)
+        nc.vector.memset(bs[0][:], 0.0)
+        nc.vector.memset(bs[1][:], 0.0)
         nc.scalar.activation(out=warm2[:], in_=warm[:], func=ACT.Tanh)
         nc.sync.dma_start(out=s_b[:], in_=s.rearrange("(e p t) -> p e t", p=P, t=4))
-        nc.sync.dma_start(out=g3_b[:], in_=g[LAST].rearrange("(p t) -> p t", t=4))
-        for e in (1, 2, 3):
+        for e in (1, 3, 2):
             load_theta(e)
         nc.sync.dma_start(out=vw[:], in_=v_words.rearrange("g p n -> p g n"))
 
@@ -107,6 +108,10 @@ def tile_calibratedlatticeensemble_d2p_kernel(
             src = tw[e][:].rearrange("p t (m u) -> p u m t", u=4)[:, u]
             if eng == "v":
                 nc.vector.tensor_copy(out=ti[e][:, u], in_=src)
+            elif eng == "g":
+                nc.gpsimd.tensor_scalar(
+                    out=ti[e][:, u], in0=src, scalar1=1.0, scalar2=0.0, op0=ALU.mult, op1=ALU.add
+                )
             else:
                 nc.scalar.copy(out=ti[e][:, u], in_=src)
 
@@ -119,94 +124,122 @@ def tile_calibratedlatticeensemble_d2p_kernel(
                 in_=ti[e][:].rearrange("p u m t -> p (u m t)"),
             )
 
+        R = HALF * E
         cc = keep.tile([P, 2, E * J], F32, name="cc")
-        lh = keep.tile([P, 2, NT, E * J], F32, name="lh")
-        mm = keep.tile([P, 2, NT * E, J], F32, name="mm")
-        pl = keep.tile([P, 2, J, NT * E], F32, name="pl")
-        pp = keep.tile([P, 4 * NT * E, 4], F32, name="pp")
-        t0 = keep.tile([P, NT, E, 8], F32, name="t0")
-        t1 = keep.tile([P, NT, E, 16], F32, name="t1")
-        r1 = keep.tile([P, NT, 3, 4], F32, name="r1")
-        r2 = keep.tile([P, NT, 3, 4], F32, name="r2")
+        lh = [keep.tile([P, 2, HALF, E * J], F32, name="lh%d" % h) for h in range(2)]
+        mm = [keep.tile([P, 2, R, J], F32, name="mm%d" % h) for h in range(2)]
+        pl = [keep.tile([P, 2, J, R], F32, name="pl%d" % h) for h in range(2)]
+        pp = [keep.tile([P, 4, R, 4], F32, name="pp%d" % h) for h in range(2)]
+        t0 = [keep.tile([P, HALF, E, 8], F32, name="t0%d" % h) for h in range(2)]
+        t1 = [keep.tile([P, HALF, E, 16], F32, name="t1%d" % h) for h in range(2)]
+        r1 = [keep.tile([P, HALF, 3, 4], F32, name="r1%d" % h) for h in range(2)]
+        r2 = [keep.tile([P, HALF, 3, 4], F32, name="r2%d" % h) for h in range(2)]
 
         nc.vector.tensor_copy(out=ident_b[:], in_=ident[:])
-        nc.vector.tensor_reduce(
-            out=mask[:], in_=ident[:, 0:36].rearrange("p (e s t) -> p e t s", e=3, s=3), axis=AX.X, op=ALU.add
-        )
         nc.vector.tensor_copy(out=cc[:, 0], in_=cal_t[:])
         nc.vector.tensor_scalar(out=cc[:, 1], in0=cal_t[:], scalar1=-1.0, scalar2=1.0, op0=ALU.mult, op1=ALU.add)
-        for e in range(3):
-            nc.gpsimd.tensor_tensor(
-                out=gt[:, e],
-                in0=gk[:].rearrange("p (m t) -> p t m", t=4),
-                in1=mask[:, e].unsqueeze(2).to_broadcast([P, 4, P]),
+
+        def low(h):
+            nc.vector.tensor_scalar(
+                out=lh[h][:, 0],
+                in0=x_t[:, HALF * h : HALF * h + HALF],
+                scalar1=2.0,
+                scalar2=1.0,
+                op0=ALU.mult,
+                op1=ALU.min,
+            )
+
+        def high(h):
+            nc.vector.scalar_tensor_tensor(
+                out=lh[h][:, 1],
+                in0=x_t[:, HALF * h : HALF * h + HALF],
+                scalar=2.0,
+                in1=lh[h][:, 0],
+                op0=ALU.mult,
+                op1=ALU.subtract,
+            )
+
+        def calibrated(h):
+            nc.vector.tensor_tensor(
+                out=mm[h][:].rearrange("p b (a e) j -> p b a (e j)", a=HALF),
+                in0=lh[h][:],
+                in1=cc[:].unsqueeze(2).to_broadcast([P, 2, HALF, E * J]),
                 op=ALU.mult,
             )
 
-        xv = x_t[:].rearrange("p (a k) -> p a k", a=NT)
-        nc.vector.tensor_scalar(out=lh[:, 0], in0=xv, scalar1=2.0, scalar2=1.0, op0=ALU.mult, op1=ALU.min)
-        nc.vector.scalar_tensor_tensor(out=lh[:, 1], in0=xv, scalar=2.0, in1=lh[:, 0], op0=ALU.mult, op1=ALU.subtract)
-        nc.vector.tensor_tensor(
-            out=mm[:].rearrange("p b (a e) j -> p b a (e j)", a=NT),
-            in0=lh[:],
-            in1=cc[:].unsqueeze(2).to_broadcast([P, 2, NT, E * J]),
-            op=ALU.mult,
-        )
-        mj = mm[:].rearrange("p b r j -> p b j r")
-        nc.vector.tensor_tensor(out=pl[:, 1, 0:4], in0=mj[:, 0, 1:9:2], in1=mj[:, 1, 1:9:2], op=ALU.add)
-        nc.vector.tensor_tensor(out=pl[:, 1, 4:9], in0=mj[:, 0, 0:9:2], in1=mj[:, 1, 0:9:2], op=ALU.add)
-        nc.vector.tensor_scalar(out=pl[:, 0], in0=pl[:, 1], scalar1=-1.0, scalar2=1.0, op0=ALU.mult, op1=ALU.add)
-        first = pl[:, :, 0:4, :].rearrange("p b q r -> p (q r) b")
-        second = pl[:, :, 5:9, :].rearrange("p b q r -> p (q r) b")
-        nc.vector.tensor_tensor(
-            out=pp[:].rearrange("p r (a b) -> p r a b", a=2),
-            in0=first.unsqueeze(3).to_broadcast([P, P, 2, 2]),
-            in1=second.unsqueeze(2).to_broadcast([P, P, 2, 2]),
-            op=ALU.mult,
-        )
-        pq = pp[:].rearrange("p (q r) c -> p q r c", q=4)
-        tail_pair = pq[:, 3].rearrange("p (a e) t -> p a e t", a=NT)
-        bsv = bs[:, :, 0:36].rearrange("p a (e s t) -> p a e s t", e=3, s=3)
-        nc.vector.tensor_copy(out=bsv[:, :, :, 0, :], in_=tail_pair[:, :, 0:3])
-        nc.vector.tensor_tensor(
-            out=t0[:].rearrange("p a e (b c) -> p (a e) b c", b=2),
-            in0=pl[:, :, 4, :].rearrange("p b r -> p r b").unsqueeze(3).to_broadcast([P, NT * E, 2, 4]),
-            in1=pq[:, 0].unsqueeze(2).to_broadcast([P, NT * E, 2, 4]),
-            op=ALU.mult,
-        )
-        nc.vector.tensor_tensor(out=r1[:], in0=tail_pair[:, :, 0:3], in1=bsv[:, :, :, 0, :], op=ALU.subtract)
-        nc.vector.tensor_tensor(
-            out=t1[:].rearrange("p a e (b c) -> p (a e) b c", b=4),
-            in0=pq[:, 1].unsqueeze(3).to_broadcast([P, NT * E, 4, 4]),
-            in1=pq[:, 2].unsqueeze(2).to_broadcast([P, NT * E, 4, 4]),
-            op=ALU.mult,
-        )
-        nc.vector.tensor_copy(out=bsv[:, :, :, 1, :], in_=r1[:])
+        def upper(h):
+            mj = mm[h][:].rearrange("p b r j -> p b j r")
+            nc.vector.tensor_tensor(out=pl[h][:, 1, 0:4], in0=mj[:, 0, 1:9:2], in1=mj[:, 1, 1:9:2], op=ALU.add)
+            nc.vector.tensor_tensor(out=pl[h][:, 1, 4:9], in0=mj[:, 0, 0:9:2], in1=mj[:, 1, 0:9:2], op=ALU.add)
+
+        def lower(h):
+            nc.vector.tensor_scalar(
+                out=pl[h][:, 0], in0=pl[h][:, 1], scalar1=-1.0, scalar2=1.0, op0=ALU.mult, op1=ALU.add
+            )
+
+        def pairs(h):
+            first = pl[h][:, :, 0:4, :].rearrange("p b q r -> p (q r) b")
+            second = pl[h][:, :, 5:9, :].rearrange("p b q r -> p (q r) b")
+            nc.vector.tensor_tensor(
+                out=pp[h][:].rearrange("p q r (a b) -> p (q r) a b", a=2),
+                in0=first.unsqueeze(3).to_broadcast([P, 4 * R, 2, 2]),
+                in1=second.unsqueeze(2).to_broadcast([P, 4 * R, 2, 2]),
+                op=ALU.mult,
+            )
+
+        tail_pair = [pp[h][:, 3].rearrange("p (a e) t -> p a e t", a=HALF) for h in range(2)]
+        bsw = [
+            bs[h][:]
+            .rearrange("p a (t w) -> p a t w", t=4)[:, :, :, 0:36]
+            .rearrange("p a t (e z) -> p a e t z", e=3)
+            for h in range(2)
+        ]
+
+        def part0(h):
+            nc.vector.tensor_copy(out=bsw[h][:, :, :, :, 0], in_=tail_pair[h][:, :, 0:3])
+
+        def rest1(h):
+            nc.vector.tensor_tensor(
+                out=r1[h][:], in0=tail_pair[h][:, :, 0:3], in1=bsw[h][:, :, :, :, 0], op=ALU.subtract
+            )
+
+        def part1(h):
+            nc.vector.tensor_copy(out=bsw[h][:, :, :, :, 1], in_=r1[h][:])
+
+        def part2(h):
+            nc.vector.tensor_tensor(
+                out=bsw[h][:, :, :, :, 2], in0=r1[h][:], in1=bsw[h][:, :, :, :, 1], op=ALU.subtract
+            )
+
+        def triple(h):
+            nc.vector.tensor_tensor(
+                out=t0[h][:].rearrange("p a e (b c) -> p (a e) b c", b=2),
+                in0=pl[h][:, :, 4, :].rearrange("p b r -> p r b").unsqueeze(3).to_broadcast([P, R, 2, 4]),
+                in1=pp[h][:, 0].unsqueeze(2).to_broadcast([P, R, 2, 4]),
+                op=ALU.mult,
+            )
+
+        def quadruple(h):
+            nc.vector.tensor_tensor(
+                out=t1[h][:].rearrange("p a e (b c) -> p (a e) b c", b=4),
+                in0=pp[h][:, 1].unsqueeze(3).to_broadcast([P, R, 4, 4]),
+                in1=pp[h][:, 2].unsqueeze(2).to_broadcast([P, R, 4, 4]),
+                op=ALU.mult,
+            )
 
         a_t = {}
 
-        def product(k):
+        def product(k, eng):
             e, h = UNITS[k]
-            rows = slice(HALF * h, HALF * h + HALF)
             a_t[k] = work.tile([P, HALF, P], F32, tag="a", name="a%d" % k)
-            nc.vector.tensor_tensor(
+            eng.tensor_tensor(
                 out=a_t[k][:].rearrange("p a (b c) -> p a b c", b=8),
-                in0=t0[:, rows, e, :].unsqueeze(3).to_broadcast([P, HALF, 8, 16]),
-                in1=t1[:, rows, e, :].unsqueeze(2).to_broadcast([P, HALF, 8, 16]),
+                in0=t0[h][:, :, e, :].unsqueeze(3).to_broadcast([P, HALF, 8, 16]),
+                in1=t1[h][:, :, e, :].unsqueeze(2).to_broadcast([P, HALF, 8, 16]),
                 op=ALU.mult,
             )
 
-        product(0)
-        nc.vector.tensor_tensor(out=r2[:], in0=r1[:], in1=bsv[:, :, :, 1, :], op=ALU.subtract)
-        nc.vector.tensor_copy(out=bsv[:, :, :, 2, :], in_=r2[:])
-
-        for t in range(4):
-            widen(0, t)
-        for u in range(4):
-            interleave(0, u, "v")
-        product(1)
-
-        bt = keep.tile([P, N], BF16, name="bt")
+        bt = keep.tile([P, NT, 4 * P], BF16, name="bt")
         at = {}
 
         def turn(k):
@@ -219,19 +252,18 @@ def tile_calibratedlatticeensemble_d2p_kernel(
             e, h = UNITS[k]
             flat = tp[:].rearrange("p a r -> p (a r)")
             if e != LAST:
-                at[k] = work.tile([P, HALF * P], F32, tag="at", name="at%d" % k)
+                at[k] = work.tile([P, HALF * P], F32, tag="at", name="at%d" % k, bufs=3)
                 nc.scalar.copy(out=at[k][:], in_=flat)
             else:
                 at[k] = work.tile([P, 4, HALF * P], F32, tag="at3", name="at%d" % k)
                 for t in range(4):
                     nc.scalar.activation(out=at[k][:, t], in_=flat, func=ACT.Copy, scale=g3[:, t : t + 1])
 
-        empty(0, turn(0))
-        for h in range(2):
-            btp = psum.tile([P, HALF, P], BF16, tag="po", name="btp%d" % h, bufs=2)
-            for i in range(HALF):
-                nc.tensor.transpose(btp[:, i, :], bs[:, HALF * h + i, :], ident_b[:])
-            nc.scalar.copy(out=bt[:, HALF * P * h : HALF * P * (h + 1)], in_=btp[:].rearrange("p a r -> p (a r)"))
+        def lay(a):
+            btp = psum.tile([P, 4, P], BF16, tag="po", name="btp%d" % a, bufs=2)
+            for t in range(4):
+                nc.tensor.transpose(btp[:, t, :], bs[a // HALF][:, a % HALF, P * t : P * (t + 1)], ident_b[:])
+            nc.scalar.copy(out=bt[:, a, :], in_=btp[:].rearrange("p t r -> p (t r)"))
 
         cb = {}
 
@@ -239,18 +271,18 @@ def tile_calibratedlatticeensemble_d2p_kernel(
             e, h = UNITS[k]
             a = HALF * h + i
             cb[(k, i)] = psum.tile([P, 4, P], F32, tag="pc", name="pc%d_%d" % (k, i), bufs=3)
-            for t in range(4):
-                if e != LAST:
-                    nc.tensor.matmul(
-                        cb[(k, i)][:, t, :],
-                        lhsT=gt[:, e, t, :],
-                        rhs=bt[:, P * a : P * (a + 1)],
-                        start=True,
-                        stop=True,
-                    )
-                else:
+            if e != LAST:
+                nc.tensor.matmul(
+                    cb[(k, i)][:].rearrange("p t r -> p (t r)"),
+                    lhsT=gl[:, e, :],
+                    rhs=bt[:, a, :],
+                    start=True,
+                    stop=True,
+                )
+            else:
+                for t in range(4):
                     nc.tensor.transpose(
-                        cb[(k, i)][:, t, :], tail_pair[:, a, e, t : t + 1].to_broadcast([P, P]), ident[:]
+                        cb[(k, i)][:, t, :], tail_pair[h][:, i, e, t : t + 1].to_broadcast([P, P]), ident[:]
                     )
 
         wg = {}
@@ -296,7 +328,7 @@ def tile_calibratedlatticeensemble_d2p_kernel(
                     stop=True,
                 )
             if i == 0:
-                hh[k] = work.tile([P, HALF, P, 4], F32, tag="hh", name="hh%d" % k)
+                hh[k] = work.tile([P, HALF, P, 4], F32, tag="hh", name="hh%d" % k, bufs=3)
             nc.scalar.activation(out=hh[k][:, i], in_=lb[:].rearrange("p t r -> p r t"), func=ACT.Tanh)
 
         def gain(k, i0, i1):
@@ -331,8 +363,8 @@ def tile_calibratedlatticeensemble_d2p_kernel(
                 lhsT_scale=fs[k][:, cols],
                 rhs=vw[:, e, :].bitcast(FP4X4),
                 rhs_scale=vs[:, e, :],
-                start=(e == 0),
-                stop=(e == E - 1),
+                start=(e == PASSES[0]),
+                stop=(e == PASSES[3]),
             )
 
         def leave(ob, a, eng):
@@ -343,76 +375,112 @@ def tile_calibratedlatticeensemble_d2p_kernel(
                 nc.scalar.copy(out=res[:], in_=ob[:])
             nc.sync.dma_start(out=out_tiles[a], in_=res[:])
 
-        nc.vector.tensor_copy(out=s_f[:], in_=s_b[:])
-        nc.vector.tensor_copy(out=g3[:], in_=g3_b[:])
-        quantize_theta(0)
-
+        for stage in (low, high, calibrated, upper, lower, pairs):
+            for h in range(2):
+                stage(h)
+        part0(0)
+        quadruple(0)
+        rest1(0)
+        triple(0)
+        part1(0)
+        product(0, nc.vector)
+        part2(0)
+        nc.vector.tensor_copy(
+            out=glt[:].rearrange("p (e w) -> p e w", e=3)[:, :, 0:12].rearrange("p e (t z) -> p e t z", z=3),
+            in_=g_b[:, 0:3].unsqueeze(3).to_broadcast([P, 3, 4, 3]),
+        )
+        nc.vector.tensor_copy(out=g3[:], in_=g_b[:, LAST])
+        for t in range(4):
+            widen(0, t)
+        for t in range(0):
+            widen(1, t)
+        tp0 = turn(0)
+        empty(0, tp0)
+        glp = psum.tile([P, 3, P], BF16, tag="po", name="glp", bufs=2)
+        for e in range(3):
+            nc.tensor.transpose(glp[:, e, :], glt[:, P * e : P * (e + 1)], ident_b[:])
+        nc.scalar.copy(out=gl[:].rearrange("p e r -> p (e r)"), in_=glp[:].rearrange("p e r -> p (e r)"))
+        for a in range(HALF):
+            lay(a)
         order = [(k, i) for k in range(8) for i in range(HALF)]
         for n in range(3):
             spread(order[n][0], order[n][1])
+        product(1, nc.vector)
+        for u in range(4):
+            interleave(0, u, THETA0)
+        nc.vector.tensor_copy(out=s_f[:], in_=s_b[:])
+        for stage in (part0, quadruple, rest1, triple, part1):
+            stage(1)
+        part2(1)
 
-        for t in range(4):
-            widen(1, t)
-        scalar_work = {
-            0: [("i", 1, 0), ("i", 1, 1), ("i", 1, 2), ("i", 1, 3), ("w", 2, 0), ("w", 2, 1)],
-            1: [("w", 2, 2), ("w", 2, 3), ("i", 2, 0), ("i", 2, 1)],
-            2: [("i", 2, 2), ("i", 2, 3), ("w", 3, 0), ("w", 3, 1), ("w", 3, 2), ("w", 3, 3)],
-            3: [("i", 3, 0), ("i", 3, 1), ("i", 3, 2), ("i", 3, 3)],
-        }
-        theta_at = {1: 1, 3: 2, 4: 3}
+        background = [("widen", 1, t) for t in range(0, 4)] + [("interleave", 1, u) for u in range(4)]
+        background[4 - 0 : 4 - 0] = [("lay", a, 0) for a in range(HALF, NT)] if WHO[1] == "s" else []
+        if WHO[1] != "s":
+            background += [("lay", a, 0) for a in range(HALF, NT)]
+        for e in (3, 2):
+            background += [("widen", e, t) for t in range(4)] + [("interleave", e, u) for u in range(4)]
+        pace = {0: 3, 1: 1, 2: 1, 3: 2, 4: 2, 5: 2}
 
-        late = {}
-        for st in range(9):
-            if st + 1 < 8:
-                tp = turn(st + 1)
+        def spare(count):
+            for n_i in range(count):
+                if background:
+                    kind, e, part = background.pop(0)
+                    if kind == "widen":
+                        widen(e, part)
+                    elif kind == "interleave":
+                        interleave(e, part, WHO[e])
+                    else:
+                        lay(e)
+
+        theta_at = {0: 0, 1: 1, 3: 3, 4: 2}
+
+        for st in range(10):
+            tp = None
             for i in range(HALF):
                 if st < 8:
                     weight(st, i)
-                if st >= 1:
+                if 1 <= st <= 8:
                     lattice(st - 1, i)
+                spare(pace.get((st, i), pace.get(st, 0)))
                 n = HALF * st + i + 3
                 if n < 32:
                     spread(order[n][0], order[n][1])
-                if st in (6, 7) and i % 2 == 1:
-                    a = 2 * (st - 6) + i // 2
+                if i == 0 and st + 1 < 8:
+                    tp = turn(st + 1)
+                if i == 1 and st + 1 < 8:
+                    empty(st + 1, tp)
+                if st in (7, 8) and i % 2 == 1:
+                    a = 2 * (st - 7) + i // 2
                     ob = psum.tile([P, Q], F32, tag="po", name="po%d" % a, bufs=2)
-                    for e in range(E):
+                    for e in PASSES:
                         mix(ob, e, a)
                     leave(ob, a, "s")
-                if st == 0 and i == 0:
-                    empty(1, tp)
-            if st >= 1 and st + 1 < 8:
-                empty(st + 1, tp)
-            for kind, e, part in scalar_work.get(st, []):
-                if kind == "w":
-                    widen(e, part)
-                else:
-                    interleave(e, part, "s")
             if st + 2 < 8:
-                product(st + 2)
-            if st >= 1 and st < 8:
-                gain(st - 1, 0, 2)
-                gain(st - 1, 2, 4)
+                product(st + 2, nc.gpsimd if st + 2 in GPS_PRODUCT else nc.vector)
+            if 2 <= st <= 8:
+                gain(st - 2, 0, HALF)
             if st in theta_at:
                 quantize_theta(theta_at[st])
             if st < 8:
                 quantize_weight(st)
-            if st >= 1 and st < 8:
-                quantize_gain(st - 1, 0, 4)
+            if 2 <= st <= 8:
+                quantize_gain(st - 2, 0, HALF)
+            if st == 9:
+                for i in range(HALF):
+                    gain(7, i, i + 1)
+                    if i >= 1:
+                        quantize_gain(7, i - 1, i)
+                quantize_gain(7, 3, 4)
 
-        for i in range(HALF):
-            gain(7, i, i + 1)
-            if i >= 1:
-                quantize_gain(7, i - 1, i)
-        quantize_gain(7, 3, 4)
         tags = ["po", "po", "pa", "pc"]
         depth = {"po": 2, "pa": 1, "pc": 3}
+        late = {}
         for i in range(HALF):
             a = HALF + i
             late[a] = psum.tile([P, Q], F32, tag=tags[i], name="po%d" % a, bufs=depth[tags[i]])
-            for e in range(3):
+            for e in PASSES[:3]:
                 mix(late[a], e, a)
         for i in range(HALF):
             a = HALF + i
-            mix(late[a], 3, a)
+            mix(late[a], PASSES[3], a)
             leave(late[a], a, "s" if i % 2 == 0 else "v")

@@ -22,7 +22,11 @@ HALF = 4
 UNITS = [(0, 0), (1, 0), (0, 1), (3, 0), (2, 0), (1, 1), (3, 1), (2, 1)]
 LAST = 3
 PASSES = [0, 1, 3, 2]
-GPS_PRODUCT = ()
+GPS_PRODUCT = (5, 6, 7)
+GPS_GAIN = (3, 4, 5, 6)
+GI = 1
+EI = 1
+TAIL_GPS = False
 THETA0 = "v"
 WHO = {1: "g", 2: "s", 3: "s"}
 
@@ -56,6 +60,8 @@ def tile_calibratedlatticeensemble_d2p_kernel(
         gl = keep.tile([P, 3, P], BF16, name="gl")
         s_f = keep.tile([P, E, 4], F32, name="s_f")
         g3 = keep.tile([P, 4], F32, name="g3")
+        s_pad = keep.tile([P, P], F32, name="s_pad")
+        s_row = keep.tile([P, P], F32, name="s_row")
 
         nc.sync.dma_start(out=x_t[:], in_=x.rearrange("(p a) e j -> p a (e j)", a=NT))
         nc.scalar.dma_start(out=cal_t[:], in_=cal.rearrange("e j -> (e j)").partition_broadcast(P))
@@ -70,6 +76,7 @@ def tile_calibratedlatticeensemble_d2p_kernel(
 
         nc.vector.memset(warm[:], 0.0)
         nc.vector.memset(glt[:], 0.0)
+        nc.vector.memset(s_pad[:], 0.0)
         nc.vector.memset(bs[0][:], 0.0)
         nc.vector.memset(bs[1][:], 0.0)
         nc.scalar.activation(out=warm2[:], in_=warm[:], func=ACT.Tanh)
@@ -103,17 +110,26 @@ def tile_calibratedlatticeensemble_d2p_kernel(
                 )
 
         def interleave(e, u, eng):
+            if u % 2:
+                return
             if u == 0:
                 ti[e] = work.tile([P, 4, P, 4], BF16, tag="ti", name="ti%d" % e, align_bytes=64)
-            src = tw[e][:].rearrange("p t (m u) -> p u m t", u=4)[:, u]
+            src = tw[e][:].rearrange("p t (m u) -> p u m t", u=4)[:, u : u + 2]
+            dst = ti[e][:, u : u + 2]
             if eng == "v":
-                nc.vector.tensor_copy(out=ti[e][:, u], in_=src)
+                nc.vector.tensor_copy(out=dst, in_=src)
             elif eng == "g":
-                nc.gpsimd.tensor_scalar(
-                    out=ti[e][:, u], in0=src, scalar1=1.0, scalar2=0.0, op0=ALU.mult, op1=ALU.add
-                )
+                if u == 2:
+                    nc.gpsimd.tensor_scalar(
+                        out=ti[e][:],
+                        in0=tw[e][:].rearrange("p t (m u) -> p u m t", u=4),
+                        scalar1=1.0,
+                        scalar2=0.0,
+                        op0=ALU.mult,
+                        op1=ALU.add,
+                    )
             else:
-                nc.scalar.copy(out=ti[e][:, u], in_=src)
+                nc.scalar.copy(out=dst, in_=src)
 
         def quantize_theta(e):
             thq[e] = keep.tile([P, O], U32, name="thq%d" % e, align_bytes=64)
@@ -239,7 +255,7 @@ def tile_calibratedlatticeensemble_d2p_kernel(
                 op=ALU.mult,
             )
 
-        bt = keep.tile([P, NT, 4 * P], BF16, name="bt")
+        bt = keep.tile([P, NT, 4, P], BF16, name="bt")
         at = {}
 
         def turn(k):
@@ -260,10 +276,10 @@ def tile_calibratedlatticeensemble_d2p_kernel(
                     nc.scalar.activation(out=at[k][:, t], in_=flat, func=ACT.Copy, scale=g3[:, t : t + 1])
 
         def lay(a):
-            btp = psum.tile([P, 4, P], BF16, tag="po", name="btp%d" % a, bufs=2)
+            btp = psum.tile([P, 4, P], BF16, tag="pl", name="btp%d" % a, bufs=2)
             for t in range(4):
                 nc.tensor.transpose(btp[:, t, :], bs[a // HALF][:, a % HALF, P * t : P * (t + 1)], ident_b[:])
-            nc.scalar.copy(out=bt[:, a, :], in_=btp[:].rearrange("p t r -> p (t r)"))
+            nc.scalar.copy(out=bt[:, a], in_=btp[:])
 
         cb = {}
 
@@ -275,7 +291,7 @@ def tile_calibratedlatticeensemble_d2p_kernel(
                 nc.tensor.matmul(
                     cb[(k, i)][:].rearrange("p t r -> p (t r)"),
                     lhsT=gl[:, e, :],
-                    rhs=bt[:, a, :],
+                    rhs=bt[:, a].rearrange("p t r -> p (t r)"),
                     start=True,
                     stop=True,
                 )
@@ -331,17 +347,19 @@ def tile_calibratedlatticeensemble_d2p_kernel(
                 hh[k] = work.tile([P, HALF, P, 4], F32, tag="hh", name="hh%d" % k, bufs=3)
             nc.scalar.activation(out=hh[k][:, i], in_=lb[:].rearrange("p t r -> p r t"), func=ACT.Tanh)
 
-        def gain(k, i0, i1):
+        def gain(k, i0, i1, gps=False):
             e, h = UNITS[k]
-            if i0 == 0:
-                ff[k] = work.tile([P, HALF, P, 4], BF16, tag="ff", name="ff%d" % k, align_bytes=64)
+            if k not in ff:
+                ff[k] = work.tile([P, HALF, P, 4], BF16, tag="ff", name="ff%d" % k, bufs=3, align_bytes=64)
                 fq[k] = keep.tile([P, HALF * P], U32, name="fq%d" % k, align_bytes=64)
                 fs[k] = keep.tile([P, HALF * P], U8, name="fs%d" % k, align_bytes=64)
             n = (i1 - i0) * P
-            nc.vector.tensor_tensor(
+            eng = nc.gpsimd if gps else nc.vector
+            factor = s_f[:, e, :] if gps else s_ps[:, 4 * e : 4 * e + 4]
+            eng.tensor_tensor(
                 out=ff[k][:, i0:i1].rearrange("p a r t -> p (a r) t"),
                 in0=hh[k][:, i0:i1].rearrange("p a r t -> p (a r) t"),
-                in1=s_f[:, e, :].unsqueeze(1).to_broadcast([P, n, 4]),
+                in1=factor.unsqueeze(1).to_broadcast([P, n, 4]),
                 op=ALU.mult,
             )
 
@@ -392,11 +410,11 @@ def tile_calibratedlatticeensemble_d2p_kernel(
         nc.vector.tensor_copy(out=g3[:], in_=g_b[:, LAST])
         for t in range(4):
             widen(0, t)
-        for t in range(0):
+        for t in range(2):
             widen(1, t)
         tp0 = turn(0)
         empty(0, tp0)
-        glp = psum.tile([P, 3, P], BF16, tag="po", name="glp", bufs=2)
+        glp = psum.tile([P, 3, P], BF16, tag="po", name="glp", bufs=1)
         for e in range(3):
             nc.tensor.transpose(glp[:, e, :], glt[:, P * e : P * (e + 1)], ident_b[:])
         nc.scalar.copy(out=gl[:].rearrange("p e r -> p (e r)"), in_=glp[:].rearrange("p e r -> p (e r)"))
@@ -409,17 +427,22 @@ def tile_calibratedlatticeensemble_d2p_kernel(
         for u in range(4):
             interleave(0, u, THETA0)
         nc.vector.tensor_copy(out=s_f[:], in_=s_b[:])
-        for stage in (part0, quadruple, rest1, triple, part1):
+        nc.vector.tensor_copy(out=s_pad[:, 0 : 4 * E], in_=s_b[:].rearrange("p e t -> p (e t)"))
+        sr = psum.tile([P, P], F32, tag="po", name="sr", bufs=1)
+        nc.tensor.transpose(sr[:], s_pad[:], ident[:])
+        nc.scalar.copy(out=s_row[:], in_=sr[:])
+        s_ps = psum.tile([P, P], F32, tag="ps", name="s_ps", bufs=1)
+        nc.tensor.transpose(s_ps[:], s_row[:], ident[:])
+        for stage in (part0, quadruple, rest1, triple, part1, part2):
             stage(1)
-        part2(1)
 
-        background = [("widen", 1, t) for t in range(0, 4)] + [("interleave", 1, u) for u in range(4)]
-        background[4 - 0 : 4 - 0] = [("lay", a, 0) for a in range(HALF, NT)] if WHO[1] == "s" else []
+        background = [("widen", 1, t) for t in range(2, 4)] + [("interleave", 1, u) for u in range(4)]
+        background[4 - 2 : 4 - 2] = [("lay", a, 0) for a in range(HALF, NT)] if WHO[1] == "s" else []
         if WHO[1] != "s":
             background += [("lay", a, 0) for a in range(HALF, NT)]
         for e in (3, 2):
             background += [("widen", e, t) for t in range(4)] + [("interleave", e, u) for u in range(4)]
-        pace = {0: 3, 1: 1, 2: 1, 3: 2, 4: 2, 5: 2}
+        pace = {0: 3, 1: 1, 2: 1, 3: 1, 4: 2, 5: 2}
 
         def spare(count):
             for n_i in range(count):
@@ -434,6 +457,7 @@ def tile_calibratedlatticeensemble_d2p_kernel(
 
         theta_at = {0: 0, 1: 1, 3: 3, 4: 2}
 
+        late = {}
         for st in range(10):
             tp = None
             for i in range(HALF):
@@ -441,46 +465,61 @@ def tile_calibratedlatticeensemble_d2p_kernel(
                     weight(st, i)
                 if 1 <= st <= 8:
                     lattice(st - 1, i)
-                spare(pace.get((st, i), pace.get(st, 0)))
+                    if i == 0 and st - 1 in GPS_GAIN:
+                        gain(st - 1, 0, 1, True)
                 n = HALF * st + i + 3
                 if n < 32:
                     spread(order[n][0], order[n][1])
                 if i == 0 and st + 1 < 8:
                     tp = turn(st + 1)
-                if i == 1 and st + 1 < 8:
+                if i == GI and st + 2 in GPS_PRODUCT:
+                    product(st + 2, nc.gpsimd)
+                if i == EI and st + 1 < 8:
                     empty(st + 1, tp)
+                spare(pace.get((st, i), pace.get(st, 0)))
                 if st in (7, 8) and i % 2 == 1:
                     a = 2 * (st - 7) + i // 2
-                    ob = psum.tile([P, Q], F32, tag="po", name="po%d" % a, bufs=2)
+                    ob = psum.tile([P, Q], F32, tag="po" if a % 2 == 0 else "pa", name="po%d" % a, bufs=1)
                     for e in PASSES:
                         mix(ob, e, a)
                     leave(ob, a, "s")
-            if st + 2 < 8:
-                product(st + 2, nc.gpsimd if st + 2 in GPS_PRODUCT else nc.vector)
+            if st + 2 < 8 and st + 2 not in GPS_PRODUCT:
+                product(st + 2, nc.vector)
             if 2 <= st <= 8:
-                gain(st - 2, 0, HALF)
+                gain(st - 2, 1 if st - 2 in GPS_GAIN else 0, HALF)
             if st in theta_at:
                 quantize_theta(theta_at[st])
             if st < 8:
                 quantize_weight(st)
             if 2 <= st <= 8:
                 quantize_gain(st - 2, 0, HALF)
+            if st == 8:
+                for e in PASSES[:3]:
+                    for a in range(HALF, HALF + 3):
+                        if e == PASSES[0]:
+                            late[a] = psum.tile([P, Q], F32, tag="pc", name="po%d" % a, bufs=3)
+                        mix(late[a], e, a)
             if st == 9:
-                for i in range(HALF):
-                    gain(7, i, i + 1)
-                    if i >= 1:
-                        quantize_gain(7, i - 1, i)
-                quantize_gain(7, 3, 4)
+                if TAIL_GPS:
+                    gain(7, 1, 2, True)
+                    gain(7, 0, 1)
+                    gain(7, 2, 3)
+                    quantize_gain(7, 0, 1)
+                    gain(7, 3, 4)
+                    quantize_gain(7, 2, 3)
+                    quantize_gain(7, 1, 2)
+                    quantize_gain(7, 3, 4)
+                else:
+                    for i in range(HALF):
+                        gain(7, i, i + 1)
+                        if i >= 1:
+                            quantize_gain(7, i - 1, i)
+                    quantize_gain(7, 3, 4)
 
-        tags = ["po", "po", "pa", "pc"]
-        depth = {"po": 2, "pa": 1, "pc": 3}
-        late = {}
         for i in range(HALF):
             a = HALF + i
-            late[a] = psum.tile([P, Q], F32, tag=tags[i], name="po%d" % a, bufs=depth[tags[i]])
-            for e in PASSES[:3]:
+            for e in PASSES[3 if i < 3 else 0 :]:
+                if e == PASSES[0]:
+                    late[a] = psum.tile([P, Q], F32, tag="po", name="po%d" % a, bufs=1)
                 mix(late[a], e, a)
-        for i in range(HALF):
-            a = HALF + i
-            mix(late[a], PASSES[3], a)
             leave(late[a], a, "s" if i % 2 == 0 else "v")

from contextlib import ExitStack

import concourse.mybir as mybir
from concourse.masks import make_identity

F32 = mybir.dt.float32
BF16 = mybir.dt.bfloat16
I32 = mybir.dt.int32
U32 = mybir.dt.uint32
U8 = mybir.dt.uint8
F8 = mybir.dt.float8_e4m3fn
FP8X4 = mybir.dt.float8_e4m3fn_x4
FP4X4 = mybir.dt.float4_e2m1fn_x4
ALU = mybir.AluOpType
ACT = mybir.ActivationFunctionType

N, E, J, NV, O, Q = 1024, 4, 9, 512, 512, 512
FLOPS = 2 * N * E * NV * O + 2 * N * E * O * Q
P = 128
NT = N // P
HALF = 4
UNITS = [(0, 0), (1, 0), (0, 1), (3, 0), (2, 0), (1, 1), (3, 1), (2, 1)]
LAST = 3
PASSES = [0, 1, 3, 2]
GPS_PRODUCT = (5, 6, 7)
GPS_GAIN = (3, 4, 5, 6)
GI = 1
EI = 1
TAIL_GPS = False
THETA0 = "v"
WHO = {1: "g", 2: "s", 3: "s"}


def tile_calibratedlatticeensemble_d2p_kernel(
    tc, x, cal, g, theta_bytes, theta_scale, s, v_words, v_scales, out
):
    nc = tc.nc
    out_tiles = out.rearrange("(p a) q -> a p q", a=NT)

    with ExitStack() as ctx:
        keep = ctx.enter_context(tc.tile_pool(name="keep", bufs=1))
        work = ctx.enter_context(tc.tile_pool(name="work", bufs=2))
        psum = ctx.enter_context(tc.psum_pool(name="psum", bufs=1))
        ctx.enter_context(tc.manual_schedule())
        x_t = keep.tile([P, NT, E * J], BF16, name="x_t")
        cal_t = keep.tile([P, E * J], BF16, name="cal_t")
        ts_t = keep.tile([P, E, 4], F32, name="ts_t")
        s_b = keep.tile([P, E, 4], BF16, name="s_b")
        g_b = keep.tile([P, E, 4], BF16, name="g_b")
        vw = keep.tile([P, E, 2 * Q], U8, name="vw", align_bytes=64)
        vs = keep.tile([P, E, Q], U8, name="vs", align_bytes=64)
        tb = [keep.tile([P, 4 * O], U8, name="tb%d" % e, align_bytes=64) for e in range(E)]

        warm = keep.tile([P, 1], F32, name="warm")
        warm2 = keep.tile([P, 1], F32, name="warm2")
        bs = [keep.tile([P, HALF, 4 * 131], BF16, name="bs%d" % h) for h in range(2)]
        glt = keep.tile([P, 3 * 140], BF16, name="glt")
        ident = keep.tile([P, P], F32, name="ident")
        ident_b = keep.tile([P, P], BF16, name="ident_b")
        gl = keep.tile([P, 3, P], BF16, name="gl")
        s_f = keep.tile([P, E, 4], F32, name="s_f")
        g3 = keep.tile([P, 4], F32, name="g3")
        s_pad = keep.tile([P, P], F32, name="s_pad")
        s_row = keep.tile([P, P], F32, name="s_row")

        nc.sync.dma_start(out=x_t[:], in_=x.rearrange("(p a) e j -> p a (e j)", a=NT))
        nc.scalar.dma_start(out=cal_t[:], in_=cal.rearrange("e j -> (e j)").partition_broadcast(P))

        def load_theta(e):
            nc.sync.dma_start(out=tb[e][:], in_=theta_bytes[e].rearrange("(p t) o -> p (t o)", t=4))

        for q in range(4):
            nc.sync.dma_start(out=ts_t[32 * q : 32 * q + 32], in_=theta_scale[:, q, :].partition_broadcast(32))
        load_theta(0)
        nc.scalar.dma_start(out=g_b[:], in_=g.rearrange("e (p t) -> p e t", t=4))

        nc.vector.memset(warm[:], 0.0)
        nc.vector.memset(glt[:], 0.0)
        nc.vector.memset(s_pad[:], 0.0)
        nc.vector.memset(bs[0][:], 0.0)
        nc.vector.memset(bs[1][:], 0.0)
        nc.scalar.activation(out=warm2[:], in_=warm[:], func=ACT.Tanh)
        nc.sync.dma_start(out=s_b[:], in_=s.rearrange("(e p t) -> p e t", p=P, t=4))
        for e in (1, 3, 2):
            load_theta(e)
        nc.sync.dma_start(out=vw[:], in_=v_words.rearrange("g p n -> p g n"))

        make_identity(nc, ident[:])
        nc.gpsimd.memset(vs[:].rearrange("p g n -> p (g n)").bitcast(I32), 0)
        for q in range(4):
            nc.sync.dma_start(
                out=vs[32 * q : 32 * q + 4].bitcast(I32),
                in_=v_scales[:, 4 * q : 4 * q + 4, :].bitcast(I32).rearrange("g r n -> r g n"),
            )

        tw = {}
        ti = {}
        thq = {}
        ths = {}

        def widen(e, t):
            if t == 0:
                tw[e] = work.tile([P, 4, O], BF16, tag="tw", name="tw%d" % e)
            for j in range(4):
                nc.scalar.activation(
                    out=tw[e][:, t, P * j : P * (j + 1)],
                    in_=tb[e][:, O * t + P * j : O * t + P * (j + 1)].bitcast(F8),
                    func=ACT.Copy,
                    scale=ts_t[:, e, j : j + 1],
                )

        def interleave(e, u, eng):
            if u % 2:
                return
            if u == 0:
                ti[e] = work.tile([P, 4, P, 4], BF16, tag="ti", name="ti%d" % e, align_bytes=64)
            src = tw[e][:].rearrange("p t (m u) -> p u m t", u=4)[:, u : u + 2]
            dst = ti[e][:, u : u + 2]
            if eng == "v":
                nc.vector.tensor_copy(out=dst, in_=src)
            elif eng == "g":
                if u == 2:
                    nc.gpsimd.tensor_scalar(
                        out=ti[e][:],
                        in0=tw[e][:].rearrange("p t (m u) -> p u m t", u=4),
                        scalar1=1.0,
                        scalar2=0.0,
                        op0=ALU.mult,
                        op1=ALU.add,
                    )
            else:
                nc.scalar.copy(out=dst, in_=src)

        def quantize_theta(e):
            thq[e] = keep.tile([P, O], U32, name="thq%d" % e, align_bytes=64)
            ths[e] = keep.tile([P, O], U8, name="ths%d" % e, align_bytes=64)
            nc.vector.quantize_mx(
                out=thq[e][:].bitcast(FP8X4),
                scales=ths[e][:],
                in_=ti[e][:].rearrange("p u m t -> p (u m t)"),
            )

        R = HALF * E
        cc = keep.tile([P, 2, E * J], F32, name="cc")
        lh = [keep.tile([P, 2, HALF, E * J], F32, name="lh%d" % h) for h in range(2)]
        mm = [keep.tile([P, 2, R, J], F32, name="mm%d" % h) for h in range(2)]
        pl = [keep.tile([P, 2, J, R], F32, name="pl%d" % h) for h in range(2)]
        pp = [keep.tile([P, 4, R, 4], F32, name="pp%d" % h) for h in range(2)]
        t0 = [keep.tile([P, HALF, E, 8], F32, name="t0%d" % h) for h in range(2)]
        t1 = [keep.tile([P, HALF, E, 16], F32, name="t1%d" % h) for h in range(2)]
        r1 = [keep.tile([P, HALF, 3, 4], F32, name="r1%d" % h) for h in range(2)]
        r2 = [keep.tile([P, HALF, 3, 4], F32, name="r2%d" % h) for h in range(2)]

        nc.vector.tensor_copy(out=ident_b[:], in_=ident[:])
        nc.vector.tensor_copy(out=cc[:, 0], in_=cal_t[:])
        nc.vector.tensor_scalar(out=cc[:, 1], in0=cal_t[:], scalar1=-1.0, scalar2=1.0, op0=ALU.mult, op1=ALU.add)

        def low(h):
            nc.vector.tensor_scalar(
                out=lh[h][:, 0],
                in0=x_t[:, HALF * h : HALF * h + HALF],
                scalar1=2.0,
                scalar2=1.0,
                op0=ALU.mult,
                op1=ALU.min,
            )

        def high(h):
            nc.vector.scalar_tensor_tensor(
                out=lh[h][:, 1],
                in0=x_t[:, HALF * h : HALF * h + HALF],
                scalar=2.0,
                in1=lh[h][:, 0],
                op0=ALU.mult,
                op1=ALU.subtract,
            )

        def calibrated(h):
            nc.vector.tensor_tensor(
                out=mm[h][:].rearrange("p b (a e) j -> p b a (e j)", a=HALF),
                in0=lh[h][:],
                in1=cc[:].unsqueeze(2).to_broadcast([P, 2, HALF, E * J]),
                op=ALU.mult,
            )

        def upper(h):
            mj = mm[h][:].rearrange("p b r j -> p b j r")
            nc.vector.tensor_tensor(out=pl[h][:, 1, 0:4], in0=mj[:, 0, 1:9:2], in1=mj[:, 1, 1:9:2], op=ALU.add)
            nc.vector.tensor_tensor(out=pl[h][:, 1, 4:9], in0=mj[:, 0, 0:9:2], in1=mj[:, 1, 0:9:2], op=ALU.add)

        def lower(h):
            nc.vector.tensor_scalar(
                out=pl[h][:, 0], in0=pl[h][:, 1], scalar1=-1.0, scalar2=1.0, op0=ALU.mult, op1=ALU.add
            )

        def pairs(h):
            first = pl[h][:, :, 0:4, :].rearrange("p b q r -> p (q r) b")
            second = pl[h][:, :, 5:9, :].rearrange("p b q r -> p (q r) b")
            nc.vector.tensor_tensor(
                out=pp[h][:].rearrange("p q r (a b) -> p (q r) a b", a=2),
                in0=first.unsqueeze(3).to_broadcast([P, 4 * R, 2, 2]),
                in1=second.unsqueeze(2).to_broadcast([P, 4 * R, 2, 2]),
                op=ALU.mult,
            )

        tail_pair = [pp[h][:, 3].rearrange("p (a e) t -> p a e t", a=HALF) for h in range(2)]
        bsw = [
            bs[h][:]
            .rearrange("p a (t w) -> p a t w", t=4)[:, :, :, 0:36]
            .rearrange("p a t (e z) -> p a e t z", e=3)
            for h in range(2)
        ]

        def part0(h):
            nc.vector.tensor_copy(out=bsw[h][:, :, :, :, 0], in_=tail_pair[h][:, :, 0:3])

        def rest1(h):
            nc.vector.tensor_tensor(
                out=r1[h][:], in0=tail_pair[h][:, :, 0:3], in1=bsw[h][:, :, :, :, 0], op=ALU.subtract
            )

        def part1(h):
            nc.vector.tensor_copy(out=bsw[h][:, :, :, :, 1], in_=r1[h][:])

        def part2(h):
            nc.vector.tensor_tensor(
                out=bsw[h][:, :, :, :, 2], in0=r1[h][:], in1=bsw[h][:, :, :, :, 1], op=ALU.subtract
            )

        def triple(h):
            nc.vector.tensor_tensor(
                out=t0[h][:].rearrange("p a e (b c) -> p (a e) b c", b=2),
                in0=pl[h][:, :, 4, :].rearrange("p b r -> p r b").unsqueeze(3).to_broadcast([P, R, 2, 4]),
                in1=pp[h][:, 0].unsqueeze(2).to_broadcast([P, R, 2, 4]),
                op=ALU.mult,
            )

        def quadruple(h):
            nc.vector.tensor_tensor(
                out=t1[h][:].rearrange("p a e (b c) -> p (a e) b c", b=4),
                in0=pp[h][:, 1].unsqueeze(3).to_broadcast([P, R, 4, 4]),
                in1=pp[h][:, 2].unsqueeze(2).to_broadcast([P, R, 4, 4]),
                op=ALU.mult,
            )

        a_t = {}

        def product(k, eng):
            e, h = UNITS[k]
            a_t[k] = work.tile([P, HALF, P], F32, tag="a", name="a%d" % k)
            eng.tensor_tensor(
                out=a_t[k][:].rearrange("p a (b c) -> p a b c", b=8),
                in0=t0[h][:, :, e, :].unsqueeze(3).to_broadcast([P, HALF, 8, 16]),
                in1=t1[h][:, :, e, :].unsqueeze(2).to_broadcast([P, HALF, 8, 16]),
                op=ALU.mult,
            )

        bt = keep.tile([P, NT, 4, P], BF16, name="bt")
        at = {}

        def turn(k):
            tp = psum.tile([P, HALF, P], F32, tag="pa", name="pa%d" % k, bufs=1)
            for i in range(HALF):
                nc.tensor.transpose(tp[:, i, :], a_t[k][:, i, :], ident[:])
            return tp

        def empty(k, tp):
            e, h = UNITS[k]
            flat = tp[:].rearrange("p a r -> p (a r)")
            if e != LAST:
                at[k] = work.tile([P, HALF * P], F32, tag="at", name="at%d" % k, bufs=3)
                nc.scalar.copy(out=at[k][:], in_=flat)
            else:
                at[k] = work.tile([P, 4, HALF * P], F32, tag="at3", name="at%d" % k)
                for t in range(4):
                    nc.scalar.activation(out=at[k][:, t], in_=flat, func=ACT.Copy, scale=g3[:, t : t + 1])

        def lay(a):
            btp = psum.tile([P, 4, P], BF16, tag="pl", name="btp%d" % a, bufs=2)
            for t in range(4):
                nc.tensor.transpose(btp[:, t, :], bs[a // HALF][:, a % HALF, P * t : P * (t + 1)], ident_b[:])
            nc.scalar.copy(out=bt[:, a], in_=btp[:])

        cb = {}

        def spread(k, i):
            e, h = UNITS[k]
            a = HALF * h + i
            cb[(k, i)] = psum.tile([P, 4, P], F32, tag="pc", name="pc%d_%d" % (k, i), bufs=3)
            if e != LAST:
                nc.tensor.matmul(
                    cb[(k, i)][:].rearrange("p t r -> p (t r)"),
                    lhsT=gl[:, e, :],
                    rhs=bt[:, a].rearrange("p t r -> p (t r)"),
                    start=True,
                    stop=True,
                )
            else:
                for t in range(4):
                    nc.tensor.transpose(
                        cb[(k, i)][:, t, :], tail_pair[h][:, i, e, t : t + 1].to_broadcast([P, P]), ident[:]
                    )

        wg = {}
        wq = {}
        wsc = {}
        hh = {}
        ff = {}
        fq = {}
        fs = {}

        def weight(k, i):
            e, h = UNITS[k]
            if i == 0:
                wg[k] = work.tile([P, HALF, P, 4], BF16, tag="wg", name="wg%d" % k, align_bytes=64)
            cols = slice(P * i, P * (i + 1))
            if e != LAST:
                right = at[k][:, cols].unsqueeze(2).to_broadcast([P, P, 4])
            else:
                right = at[k][:, :, cols].rearrange("p t r -> p r t")
            nc.vector.tensor_tensor(
                out=wg[k][:, i], in0=cb[(k, i)][:].rearrange("p t r -> p r t"), in1=right, op=ALU.mult
            )

        def quantize_weight(k):
            wq[k] = work.tile([P, HALF * P], U32, tag="wq", name="wq%d" % k, align_bytes=64)
            wsc[k] = work.tile([P, HALF * P], U8, tag="wsc", name="wsc%d" % k, align_bytes=64)
            nc.vector.quantize_mx(
                out=wq[k][:].bitcast(FP8X4), scales=wsc[k][:], in_=wg[k][:].rearrange("p a r t -> p (a r t)")
            )

        def lattice(k, i):
            e, h = UNITS[k]
            lb = psum.tile([P, 4, P], F32, tag="pl", name="pl%d_%d" % (k, i), bufs=2)
            cols = slice(P * i, P * (i + 1))
            for u in range(4):
                nc.tensor.matmul_mx(
                    out=lb[:, u, :],
                    lhsT=thq[e][:, P * u : P * (u + 1)].bitcast(FP8X4),
                    lhsT_scale=ths[e][:, P * u : P * (u + 1)],
                    rhs=wq[k][:, cols].bitcast(FP8X4),
                    rhs_scale=wsc[k][:, cols],
                    start=True,
                    stop=True,
                )
            if i == 0:
                hh[k] = work.tile([P, HALF, P, 4], F32, tag="hh", name="hh%d" % k, bufs=3)
            nc.scalar.activation(out=hh[k][:, i], in_=lb[:].rearrange("p t r -> p r t"), func=ACT.Tanh)

        def gain(k, i0, i1, gps=False):
            e, h = UNITS[k]
            if k not in ff:
                ff[k] = work.tile([P, HALF, P, 4], BF16, tag="ff", name="ff%d" % k, bufs=3, align_bytes=64)
                fq[k] = keep.tile([P, HALF * P], U32, name="fq%d" % k, align_bytes=64)
                fs[k] = keep.tile([P, HALF * P], U8, name="fs%d" % k, align_bytes=64)
            n = (i1 - i0) * P
            eng = nc.gpsimd if gps else nc.vector
            factor = s_f[:, e, :] if gps else s_ps[:, 4 * e : 4 * e + 4]
            eng.tensor_tensor(
                out=ff[k][:, i0:i1].rearrange("p a r t -> p (a r) t"),
                in0=hh[k][:, i0:i1].rearrange("p a r t -> p (a r) t"),
                in1=factor.unsqueeze(1).to_broadcast([P, n, 4]),
                op=ALU.mult,
            )

        def quantize_gain(k, i0, i1):
            nc.vector.quantize_mx(
                out=fq[k][:, P * i0 : P * i1].bitcast(FP8X4),
                scales=fs[k][:, P * i0 : P * i1],
                in_=ff[k][:, i0:i1].rearrange("p a r t -> p (a r t)"),
            )

        unit_of = {UNITS[k]: k for k in range(len(UNITS))}

        def mix(ob, e, a):
            k = unit_of[(e, a // HALF)]
            cols = slice(P * (a % HALF), P * (a % HALF + 1))
            nc.tensor.matmul_mx(
                out=ob[:],
                lhsT=fq[k][:, cols].bitcast(FP8X4),
                lhsT_scale=fs[k][:, cols],
                rhs=vw[:, e, :].bitcast(FP4X4),
                rhs_scale=vs[:, e, :],
                start=(e == PASSES[0]),
                stop=(e == PASSES[3]),
            )

        def leave(ob, a, eng):
            res = work.tile([P, Q], F32, tag="res", name="res%d" % a, bufs=4)
            if eng == "v":
                nc.vector.tensor_copy(out=res[:], in_=ob[:])
            else:
                nc.scalar.copy(out=res[:], in_=ob[:])
            nc.sync.dma_start(out=out_tiles[a], in_=res[:])

        for stage in (low, high, calibrated, upper, lower, pairs):
            for h in range(2):
                stage(h)
        part0(0)
        quadruple(0)
        rest1(0)
        triple(0)
        part1(0)
        product(0, nc.vector)
        part2(0)
        nc.vector.tensor_copy(
            out=glt[:].rearrange("p (e w) -> p e w", e=3)[:, :, 0:12].rearrange("p e (t z) -> p e t z", z=3),
            in_=g_b[:, 0:3].unsqueeze(3).to_broadcast([P, 3, 4, 3]),
        )
        nc.vector.tensor_copy(out=g3[:], in_=g_b[:, LAST])
        for t in range(4):
            widen(0, t)
        for t in range(2):
            widen(1, t)
        tp0 = turn(0)
        empty(0, tp0)
        glp = psum.tile([P, 3, P], BF16, tag="po", name="glp", bufs=1)
        for e in range(3):
            nc.tensor.transpose(glp[:, e, :], glt[:, P * e : P * (e + 1)], ident_b[:])
        nc.scalar.copy(out=gl[:].rearrange("p e r -> p (e r)"), in_=glp[:].rearrange("p e r -> p (e r)"))
        for a in range(HALF):
            lay(a)
        order = [(k, i) for k in range(8) for i in range(HALF)]
        for n in range(3):
            spread(order[n][0], order[n][1])
        product(1, nc.vector)
        for u in range(4):
            interleave(0, u, THETA0)
        nc.vector.tensor_copy(out=s_f[:], in_=s_b[:])
        nc.vector.tensor_copy(out=s_pad[:, 0 : 4 * E], in_=s_b[:].rearrange("p e t -> p (e t)"))
        sr = psum.tile([P, P], F32, tag="po", name="sr", bufs=1)
        nc.tensor.transpose(sr[:], s_pad[:], ident[:])
        nc.scalar.copy(out=s_row[:], in_=sr[:])
        s_ps = psum.tile([P, P], F32, tag="ps", name="s_ps", bufs=1)
        nc.tensor.transpose(s_ps[:], s_row[:], ident[:])
        for stage in (part0, quadruple, rest1, triple, part1, part2):
            stage(1)

        background = [("widen", 1, t) for t in range(2, 4)] + [("interleave", 1, u) for u in range(4)]
        background[4 - 2 : 4 - 2] = [("lay", a, 0) for a in range(HALF, NT)] if WHO[1] == "s" else []
        if WHO[1] != "s":
            background += [("lay", a, 0) for a in range(HALF, NT)]
        for e in (3, 2):
            background += [("widen", e, t) for t in range(4)] + [("interleave", e, u) for u in range(4)]
        pace = {0: 3, 1: 1, 2: 1, 3: 1, 4: 2, 5: 2}

        def spare(count):
            for n_i in range(count):
                if background:
                    kind, e, part = background.pop(0)
                    if kind == "widen":
                        widen(e, part)
                    elif kind == "interleave":
                        interleave(e, part, WHO[e])
                    else:
                        lay(e)

        theta_at = {0: 0, 1: 1, 3: 3, 4: 2}

        late = {}
        for st in range(10):
            tp = None
            for i in range(HALF):
                if st < 8:
                    weight(st, i)
                if 1 <= st <= 8:
                    lattice(st - 1, i)
                    if i == 0 and st - 1 in GPS_GAIN:
                        gain(st - 1, 0, 1, True)
                n = HALF * st + i + 3
                if n < 32:
                    spread(order[n][0], order[n][1])
                if i == 0 and st + 1 < 8:
                    tp = turn(st + 1)
                if i == GI and st + 2 in GPS_PRODUCT:
                    product(st + 2, nc.gpsimd)
                if i == EI and st + 1 < 8:
                    empty(st + 1, tp)
                spare(pace.get((st, i), pace.get(st, 0)))
                if st in (7, 8) and i % 2 == 1:
                    a = 2 * (st - 7) + i // 2
                    ob = psum.tile([P, Q], F32, tag="po" if a % 2 == 0 else "pa", name="po%d" % a, bufs=1)
                    for e in PASSES:
                        mix(ob, e, a)
                    leave(ob, a, "s")
            if st + 2 < 8 and st + 2 not in GPS_PRODUCT:
                product(st + 2, nc.vector)
            if 2 <= st <= 8:
                gain(st - 2, 1 if st - 2 in GPS_GAIN else 0, HALF)
            if st in theta_at:
                quantize_theta(theta_at[st])
            if st < 8:
                quantize_weight(st)
            if 2 <= st <= 8:
                quantize_gain(st - 2, 0, HALF)
            if st == 8:
                for e in PASSES[:3]:
                    for a in range(HALF, HALF + 3):
                        if e == PASSES[0]:
                            late[a] = psum.tile([P, Q], F32, tag="pc", name="po%d" % a, bufs=3)
                        mix(late[a], e, a)
            if st == 9:
                if TAIL_GPS:
                    gain(7, 1, 2, True)
                    gain(7, 0, 1)
                    gain(7, 2, 3)
                    quantize_gain(7, 0, 1)
                    gain(7, 3, 4)
                    quantize_gain(7, 2, 3)
                    quantize_gain(7, 1, 2)
                    quantize_gain(7, 3, 4)
                else:
                    for i in range(HALF):
                        gain(7, i, i + 1)
                        if i >= 1:
                            quantize_gain(7, i - 1, i)
                    quantize_gain(7, 3, 4)

        for i in range(HALF):
            a = HALF + i
            for e in PASSES[3 if i < 3 else 0 :]:
                if e == PASSES[0]:
                    late[a] = psum.tile([P, Q], F32, tag="po", name="po%d" % a, bufs=1)
                mix(late[a], e, a)
            leave(late[a], a, "s" if i % 2 == 0 else "v")
